import numpy as np
import ml_dtypes

BF16 = ml_dtypes.bfloat16


def bf(x):
    return np.asarray(x, np.float32).astype(BF16)


def f32(x):
    return np.asarray(x, np.float32)


def f64(x):
    return np.asarray(x).astype(np.float64)


def striped(idx):
    return np.tile(idx.reshape(-1, 16).T, (8, 1))


S, K, M, N = 512, 128, 128, 256


def setup_inputs():
    return {"base": bf(np.random.standard_normal((M, S))), "x": bf(np.random.standard_normal((K, N))), "w": bf(np.random.standard_normal((K, M)) / np.sqrt(K)), "s": f32(0.5 + np.random.random_sample((M, 1))), "b": f32(0.5 * np.random.standard_normal((M, 1))), "offs": striped(np.random.permutation(S)[:N])}


def reference(base, x, w, s, b, offs):
    idx = offs[:16].T.reshape(-1)
    z = f64(base).copy()
    z[:, idx] = f64(w).T @ f64(x)
    return z * f64(s) + f64(b)

@@ -1,0 +1,44 @@
+import concourse.mybir as mybir
+from concourse.masks import make_identity
+
+BF16, F32, U16 = mybir.dt.bfloat16, mybir.dt.float32, mybir.dt.uint16
+MULT, ADD = mybir.AluOpType.mult, mybir.AluOpType.add
+
+P = 128
+S = 512
+N = 256
+
+FLOPS = 2 * P * P * N
+
+
+def tile_scatter_matmul_kernel(tc, base, x, w, s, b, offs, out):
+    nc = tc.nc
+    with (
+        tc.tile_pool(name="held", bufs=1) as held,
+        tc.psum_pool(name="psum", bufs=1) as psum,
+    ):
+        offsets = held.tile([P, N // 16], U16, name="offsets")
+        nc.sync.dma_start(offsets[:], offs)
+
+        base_tile = held.tile([P, S], BF16, name="base_tile")
+        nc.scalar.dma_start(base_tile[:], base)
+        weights = held.tile([P, P], BF16, name="weights")
+        nc.sync.dma_start(weights[:], w)
+        moving = held.tile([P, N], BF16, name="moving")
+        nc.sync.dma_start(moving[:], x)
+        gain = held.tile([P, 1], F32, name="gain")
+        nc.scalar.dma_start(gain[:], s)
+        shift = held.tile([P, 1], F32, name="shift")
+        nc.scalar.dma_start(shift[:], b)
+
+        ident = held.tile([P, P], BF16, name="ident")
+        make_identity(nc, ident[:])
+
+        window = psum.tile([P, S], F32, name="window")
+        nc.tensor.matmul(window[:], ident[:], base_tile[:], start=True, stop=True)
+
+        nc.tensor.matmul(window[:].indirect(offsets[:]), weights[:], moving[:], start=True, stop=True)
+
+        result = held.tile([P, S], F32, name="result")
+        nc.vector.tensor_scalar(result[:], window[:], gain[:, 0:1], shift[:, 0:1], MULT, ADD)
+        nc.sync.dma_start(out, result[:])

@@ -3,10 +3,12 @@ from concourse.masks import make_identity
 
 BF16, F32, U16 = mybir.dt.bfloat16, mybir.dt.float32, mybir.dt.uint16
 MULT, ADD = mybir.AluOpType.mult, mybir.AluOpType.add
+IDENTITY = mybir.ActivationFunctionType.Identity
 
 P = 128
 S = 512
 N = 256
+HALF = S // 2
 
 FLOPS = 2 * P * P * N
 
@@ -31,6 +33,10 @@ def tile_scatter_matmul_kernel(tc, base, x, w, s, b, offs, out):
         shift = held.tile([P, 1], F32, name="shift")
         nc.scalar.dma_start(shift[:], b)
 
+        primer = held.tile([P, 1], F32, name="primer")
+        nc.vector.memset(primer[:], 0.0)
+        nc.scalar.activation(primer[:], primer[:], IDENTITY)
+
         ident = held.tile([P, P], BF16, name="ident")
         make_identity(nc, ident[:])
 
@@ -39,6 +45,9 @@ def tile_scatter_matmul_kernel(tc, base, x, w, s, b, offs, out):
 
         nc.tensor.matmul(window[:].indirect(offsets[:]), weights[:], moving[:], start=True, stop=True)
 
-        result = held.tile([P, S], F32, name="result")
-        nc.vector.tensor_scalar(result[:], window[:], gain[:, 0:1], shift[:, 0:1], MULT, ADD)
-        nc.sync.dma_start(out, result[:])
+        left = held.tile([P, HALF], F32, name="left")
+        nc.vector.tensor_scalar(left[:], window[:, 0:HALF], gain[:, 0:1], shift[:, 0:1], MULT, ADD)
+        nc.sync.dma_start(out[:, 0:HALF], left[:])
+        right = held.tile([P, HALF], F32, name="right")
+        nc.scalar.activation(right[:], window[:, HALF:S], IDENTITY, bias=shift[:, 0:1], scale=gain[:, 0:1])
+        nc.scalar.dma_start(out[:, HALF:S], right[:])

@@ -19,17 +19,19 @@ def tile_scatter_matmul_kernel(tc, base, x, w, s, b, offs, out):
         tc.tile_pool(name="held", bufs=1) as held,
         tc.psum_pool(name="psum", bufs=1) as psum,
     ):
+        base_left = held.tile([P, HALF], BF16, name="base_left")
+        nc.sync.dma_start(base_left[:], base[:, 0:HALF])
+        base_right = held.tile([P, HALF], BF16, name="base_right")
+        nc.scalar.dma_start(base_right[:], base[:, HALF:S])
+
         offsets = held.tile([P, N // 16], U16, name="offsets")
         nc.sync.dma_start(offsets[:], offs)
-
-        base_tile = held.tile([P, S], BF16, name="base_tile")
-        nc.scalar.dma_start(base_tile[:], base)
         weights = held.tile([P, P], BF16, name="weights")
-        nc.sync.dma_start(weights[:], w)
+        nc.scalar.dma_start(weights[:], w)
         moving = held.tile([P, N], BF16, name="moving")
         nc.sync.dma_start(moving[:], x)
         gain = held.tile([P, 1], F32, name="gain")
-        nc.scalar.dma_start(gain[:], s)
+        nc.sync.dma_start(gain[:], s)
         shift = held.tile([P, 1], F32, name="shift")
         nc.scalar.dma_start(shift[:], b)
 
@@ -41,7 +43,8 @@ def tile_scatter_matmul_kernel(tc, base, x, w, s, b, offs, out):
         make_identity(nc, ident[:])
 
         window = psum.tile([P, S], F32, name="window")
-        nc.tensor.matmul(window[:], ident[:], base_tile[:], start=True, stop=True)
+        nc.tensor.matmul(window[:, 0:HALF], ident[:], base_left[:], start=True, stop=True)
+        nc.tensor.matmul(window[:, HALF:S], ident[:], base_right[:], start=True, stop=True)
 
         nc.tensor.matmul(window[:].indirect(offsets[:]), weights[:], moving[:], start=True, stop=True)
 

@@ -19,21 +19,19 @@ def tile_scatter_matmul_kernel(tc, base, x, w, s, b, offs, out):
         tc.tile_pool(name="held", bufs=1) as held,
         tc.psum_pool(name="psum", bufs=1) as psum,
     ):
-        base_left = held.tile([P, HALF], BF16, name="base_left")
-        nc.sync.dma_start(base_left[:], base[:, 0:HALF])
-        base_right = held.tile([P, HALF], BF16, name="base_right")
-        nc.scalar.dma_start(base_right[:], base[:, HALF:S])
+        base_tile = held.tile([P, S], BF16, name="base_tile")
+        nc.scalar.dma_start(base_tile[:], base)
 
-        offsets = held.tile([P, N // 16], U16, name="offsets")
-        nc.sync.dma_start(offsets[:], offs)
-        weights = held.tile([P, P], BF16, name="weights")
-        nc.scalar.dma_start(weights[:], w)
-        moving = held.tile([P, N], BF16, name="moving")
-        nc.sync.dma_start(moving[:], x)
         gain = held.tile([P, 1], F32, name="gain")
         nc.sync.dma_start(gain[:], s)
         shift = held.tile([P, 1], F32, name="shift")
-        nc.scalar.dma_start(shift[:], b)
+        nc.sync.dma_start(shift[:], b)
+        offsets = held.tile([P, N // 16], U16, name="offsets")
+        nc.sync.dma_start(offsets[:], offs)
+        weights = held.tile([P, P], BF16, name="weights")
+        nc.sync.dma_start(weights[:], w)
+        moving = held.tile([P, N], BF16, name="moving")
+        nc.sync.dma_start(moving[:], x)
 
         primer = held.tile([P, 1], F32, name="primer")
         nc.vector.memset(primer[:], 0.0)
@@ -43,8 +41,7 @@ def tile_scatter_matmul_kernel(tc, base, x, w, s, b, offs, out):
         make_identity(nc, ident[:])
 
         window = psum.tile([P, S], F32, name="window")
-        nc.tensor.matmul(window[:, 0:HALF], ident[:], base_left[:], start=True, stop=True)
-        nc.tensor.matmul(window[:, HALF:S], ident[:], base_right[:], start=True, stop=True)
+        nc.tensor.matmul(window[:], ident[:], base_tile[:], start=True, stop=True)
 
         nc.tensor.matmul(window[:].indirect(offsets[:]), weights[:], moving[:], start=True, stop=True)
 

@@ -9,6 +9,7 @@ P = 128
 S = 512
 N = 256
 HALF = S // 2
+WARMING = 3
 
 FLOPS = 2 * P * P * N
 
@@ -19,19 +20,25 @@ def tile_scatter_matmul_kernel(tc, base, x, w, s, b, offs, out):
         tc.tile_pool(name="held", bufs=1) as held,
         tc.psum_pool(name="psum", bufs=1) as psum,
     ):
-        base_tile = held.tile([P, S], BF16, name="base_tile")
-        nc.scalar.dma_start(base_tile[:], base)
-
-        gain = held.tile([P, 1], F32, name="gain")
-        nc.sync.dma_start(gain[:], s)
-        shift = held.tile([P, 1], F32, name="shift")
-        nc.sync.dma_start(shift[:], b)
         offsets = held.tile([P, N // 16], U16, name="offsets")
         nc.sync.dma_start(offsets[:], offs)
+
+        base_tile = held.tile([P, S], BF16, name="base_tile")
+        nc.scalar.dma_start(base_tile[:], base)
         weights = held.tile([P, P], BF16, name="weights")
         nc.sync.dma_start(weights[:], w)
         moving = held.tile([P, N], BF16, name="moving")
         nc.sync.dma_start(moving[:], x)
+        gain = held.tile([P, 1], F32, name="gain")
+        nc.scalar.dma_start(gain[:], s)
+        shift = held.tile([P, 1], F32, name="shift")
+        nc.scalar.dma_start(shift[:], b)
+
+        zeros = held.tile([P, S], BF16, name="zeros")
+        nc.vector.memset(zeros[:], 0.0)
+        unread = psum.tile([P, S], F32, name="unread")
+        for i in range(WARMING):
+            nc.tensor.matmul(unread[:], zeros[:, 0:P], zeros[:], start=True, stop=True)
 
         primer = held.tile([P, 1], F32, name="primer")
         nc.vector.memset(primer[:], 0.0)

@@ -34,11 +34,14 @@ def tile_scatter_matmul_kernel(tc, base, x, w, s, b, offs, out):
         shift = held.tile([P, 1], F32, name="shift")
         nc.scalar.dma_start(shift[:], b)
 
-        zeros = held.tile([P, S], BF16, name="zeros")
+        zeros = held.tile([P, P], BF16, name="zeros")
         nc.vector.memset(zeros[:], 0.0)
+        zeros_repeated = zeros[:].unsqueeze(1).to_broadcast([P, S // P, P])
         unread = psum.tile([P, S], F32, name="unread")
         for i in range(WARMING):
-            nc.tensor.matmul(unread[:], zeros[:, 0:P], zeros[:], start=True, stop=True)
+            nc.tensor.matmul(
+                unread[:].rearrange("p (r c) -> p r c", c=P), zeros[:], zeros_repeated, start=True, stop=True
+            )
 
         primer = held.tile([P, 1], F32, name="primer")
         nc.vector.memset(primer[:], 0.0)

@@ -2,7 +2,6 @@ import concourse.mybir as mybir
 from concourse.masks import make_identity
 
 BF16, F32, U16 = mybir.dt.bfloat16, mybir.dt.float32, mybir.dt.uint16
-MULT, ADD = mybir.AluOpType.mult, mybir.AluOpType.add
 IDENTITY = mybir.ActivationFunctionType.Identity
 
 P = 128
@@ -56,7 +55,7 @@ def tile_scatter_matmul_kernel(tc, base, x, w, s, b, offs, out):
         nc.tensor.matmul(window[:].indirect(offsets[:]), weights[:], moving[:], start=True, stop=True)
 
         left = held.tile([P, HALF], F32, name="left")
-        nc.vector.tensor_scalar(left[:], window[:, 0:HALF], gain[:, 0:1], shift[:, 0:1], MULT, ADD)
+        nc.scalar.activation(left[:], window[:, 0:HALF], IDENTITY, bias=shift[:, 0:1], scale=gain[:, 0:1])
         nc.sync.dma_start(out[:, 0:HALF], left[:])
         right = held.tile([P, HALF], F32, name="right")
         nc.scalar.activation(right[:], window[:, HALF:S], IDENTITY, bias=shift[:, 0:1], scale=gain[:, 0:1])

import concourse.mybir as mybir
from concourse.masks import make_identity

BF16, F32, U16 = mybir.dt.bfloat16, mybir.dt.float32, mybir.dt.uint16
IDENTITY = mybir.ActivationFunctionType.Identity

P = 128
S = 512
N = 256
HALF = S // 2
WARMING = 3

FLOPS = 2 * P * P * N


def tile_scatter_matmul_kernel(tc, base, x, w, s, b, offs, out):
    nc = tc.nc
    with (
        tc.tile_pool(name="held", bufs=1) as held,
        tc.psum_pool(name="psum", bufs=1) as psum,
    ):
        offsets = held.tile([P, N // 16], U16, name="offsets")
        nc.sync.dma_start(offsets[:], offs)

        base_tile = held.tile([P, S], BF16, name="base_tile")
        nc.scalar.dma_start(base_tile[:], base)
        weights = held.tile([P, P], BF16, name="weights")
        nc.sync.dma_start(weights[:], w)
        moving = held.tile([P, N], BF16, name="moving")
        nc.sync.dma_start(moving[:], x)
        gain = held.tile([P, 1], F32, name="gain")
        nc.scalar.dma_start(gain[:], s)
        shift = held.tile([P, 1], F32, name="shift")
        nc.scalar.dma_start(shift[:], b)

        zeros = held.tile([P, P], BF16, name="zeros")
        nc.vector.memset(zeros[:], 0.0)
        zeros_repeated = zeros[:].unsqueeze(1).to_broadcast([P, S // P, P])
        unread = psum.tile([P, S], F32, name="unread")
        for i in range(WARMING):
            nc.tensor.matmul(
                unread[:].rearrange("p (r c) -> p r c", c=P), zeros[:], zeros_repeated, start=True, stop=True
            )

        primer = held.tile([P, 1], F32, name="primer")
        nc.vector.memset(primer[:], 0.0)
        nc.scalar.activation(primer[:], primer[:], IDENTITY)

        ident = held.tile([P, P], BF16, name="ident")
        make_identity(nc, ident[:])

        window = psum.tile([P, S], F32, name="window")
        nc.tensor.matmul(window[:], ident[:], base_tile[:], start=True, stop=True)

        nc.tensor.matmul(window[:].indirect(offsets[:]), weights[:], moving[:], start=True, stop=True)

        left = held.tile([P, HALF], F32, name="left")
        nc.scalar.activation(left[:], window[:, 0:HALF], IDENTITY, bias=shift[:, 0:1], scale=gain[:, 0:1])
        nc.sync.dma_start(out[:, 0:HALF], left[:])
        right = held.tile([P, HALF], F32, name="right")
        nc.scalar.activation(right[:], window[:, HALF:S], IDENTITY, bias=shift[:, 0:1], scale=gain[:, 0:1])
        nc.scalar.dma_start(out[:, HALF:S], right[:])
